import numpy as np
import ml_dtypes

BF16 = ml_dtypes.bfloat16


def bf(x):
    return np.asarray(x, np.float32).astype(BF16)


def f32(x):
    return np.asarray(x, np.float32)


def f64(x):
    return np.asarray(x).astype(np.float64)


def striped(idx):
    return np.concatenate([l.reshape(-1, 16).T for l in idx])


def rows(idx, k):
    return np.tile(np.repeat(idx, 16, axis=0), (k // (16 * 8), 1))


def look(tab, idx):
    return np.take_along_axis(f64(tab), rows(idx, len(tab)), axis=1)


K, S, V, N = 512, 2048, 1024, 1024


def silu(v):
    return v / (1.0 + np.exp(-v))


def setup_inputs():
    return {"tab": f32(np.random.standard_normal((2, K, S))), "y": f32(np.random.standard_normal((K, V))), "offs": striped(np.stack([np.random.permutation(S)[:N] for _ in range(8)]))}


def reference(tab, y, offs):
    idx = np.stack([g.T.reshape(-1) for g in np.split(offs, 8)])
    x = (np.minimum(look(tab[0], idx), f64(y))) * (silu(look(tab[1], idx)))
    return x

@@ -1,0 +1,48 @@
+import concourse.mybir as mybir
+
+F32 = mybir.dt.float32
+U16 = mybir.dt.uint16
+MIN = mybir.AluOpType.min
+MULT = mybir.AluOpType.mult
+SILU = mybir.ActivationFunctionType.Silu
+
+P = 128
+LIST_ROWS = 16
+PIECE = 512
+
+
+def tile_lookup_vg_minsilu_out_kernel(tc, tab, y, offs, out):
+    nc = tc.nc
+    rows, places = tab.shape[1], tab.shape[2]
+    n = y.shape[1]
+    blocks = rows // P
+
+    with (
+        tc.tile_pool(name="lists", bufs=1) as lists,
+        tc.tile_pool(name="held", bufs=blocks) as held,
+    ):
+        offsets = lists.tile([P, n // LIST_ROWS], U16, name="offsets")
+        nc.sync.dma_start(offsets[:], offs)
+
+        loaded = []
+        for b in range(blocks):
+            block = slice(b * P, (b + 1) * P)
+            gates = held.tile([P, places], F32, name="gates")
+            values = held.tile([P, places], F32, name="values")
+            stream = held.tile([P, n], F32, name="stream")
+            nc.sync.dma_start(gates[:], tab[1, block, :])
+            nc.sync.dma_start(values[:], tab[0, block, :])
+            nc.sync.dma_start(stream[:], y[block, :])
+            loaded.append((gates, values, stream))
+
+        for b, (gates, values, stream) in enumerate(loaded):
+            gated = held.tile([P, n], F32, name="gated")
+            clipped = held.tile([P, n], F32, name="clipped")
+            product = held.tile([P, n], F32, name="product")
+            for start in range(0, n, PIECE):
+                cols = slice(start, start + PIECE)
+                piece = offsets[:, start // LIST_ROWS : (start + PIECE) // LIST_ROWS]
+                nc.scalar.activation(gated[:, cols], gates[:].indirect(piece), SILU)
+                nc.vector.tensor_tensor(clipped[:, cols], values[:].indirect(piece), stream[:, cols], MIN)
+                nc.vector.tensor_tensor(product[:, cols], clipped[:, cols], gated[:, cols], MULT)
+            nc.sync.dma_start(out[b * P : (b + 1) * P, :], product[:])

@@ -16,6 +16,7 @@ def tile_lookup_vg_minsilu_out_kernel(tc, tab, y, offs, out):
     rows, places = tab.shape[1], tab.shape[2]
     n = y.shape[1]
     blocks = rows // P
+    pieces = [slice(start, start + PIECE) for start in range(0, n, PIECE)]
 
     with (
         tc.tile_pool(name="lists", bufs=1) as lists,
@@ -27,22 +28,27 @@ def tile_lookup_vg_minsilu_out_kernel(tc, tab, y, offs, out):
         loaded = []
         for b in range(blocks):
             block = slice(b * P, (b + 1) * P)
-            gates = held.tile([P, places], F32, name="gates")
             values = held.tile([P, places], F32, name="values")
+            gates = held.tile([P, places], F32, name="gates")
             stream = held.tile([P, n], F32, name="stream")
-            nc.sync.dma_start(gates[:], tab[1, block, :])
+            early = n - PIECE if b == blocks - 1 else n
             nc.sync.dma_start(values[:], tab[0, block, :])
-            nc.sync.dma_start(stream[:], y[block, :])
-            loaded.append((gates, values, stream))
+            nc.sync.dma_start(stream[:, :early], y[block, :early])
+            nc.sync.dma_start(gates[:], tab[1, block, :])
+            if early < n:
+                nc.sync.dma_start(stream[:, early:], y[block, early:])
+            loaded.append((values, gates, stream))
 
-        for b, (gates, values, stream) in enumerate(loaded):
-            gated = held.tile([P, n], F32, name="gated")
+        for b, (values, gates, stream) in enumerate(loaded):
+            block = slice(b * P, (b + 1) * P)
             clipped = held.tile([P, n], F32, name="clipped")
+            gated = held.tile([P, n], F32, name="gated")
             product = held.tile([P, n], F32, name="product")
-            for start in range(0, n, PIECE):
-                cols = slice(start, start + PIECE)
-                piece = offsets[:, start // LIST_ROWS : (start + PIECE) // LIST_ROWS]
-                nc.scalar.activation(gated[:, cols], gates[:].indirect(piece), SILU)
-                nc.vector.tensor_tensor(clipped[:, cols], values[:].indirect(piece), stream[:, cols], MIN)
+            for cols in pieces:
+                entries = offsets[:, cols.start // LIST_ROWS : cols.stop // LIST_ROWS]
+                nc.vector.tensor_tensor(clipped[:, cols], values[:].indirect(entries), stream[:, cols], MIN)
+                nc.scalar.activation(gated[:, cols], gates[:].indirect(entries), SILU)
+            for cols in pieces:
                 nc.vector.tensor_tensor(product[:, cols], clipped[:, cols], gated[:, cols], MULT)
-            nc.sync.dma_start(out[b * P : (b + 1) * P, :], product[:])
+            for cols in pieces if b == blocks - 1 else [slice(0, n)]:
+                nc.sync.dma_start(out[block, cols], product[:, cols])

@@ -16,39 +16,43 @@ def tile_lookup_vg_minsilu_out_kernel(tc, tab, y, offs, out):
     rows, places = tab.shape[1], tab.shape[2]
     n = y.shape[1]
     blocks = rows // P
+    last = blocks - 1
     pieces = [slice(start, start + PIECE) for start in range(0, n, PIECE)]
+    y_blocks = y.rearrange("(b p) j -> p b j", p=P)
+    out_blocks = out.rearrange("(b p) j -> p b j", p=P)
 
     with (
-        tc.tile_pool(name="lists", bufs=1) as lists,
-        tc.tile_pool(name="held", bufs=blocks) as held,
+        tc.tile_pool(name="held", bufs=1) as held,
+        tc.tile_pool(name="per_block", bufs=blocks) as per_block,
     ):
-        offsets = lists.tile([P, n // LIST_ROWS], U16, name="offsets")
+        offsets = held.tile([P, n // LIST_ROWS], U16, name="offsets")
+        stream = held.tile([P, blocks, n], F32, name="stream")
+        product = held.tile([P, blocks, n], F32, name="product")
         nc.sync.dma_start(offsets[:], offs)
+        nc.scalar.dma_start(stream[:, :last, :], y_blocks[:, :last, :])
 
-        loaded = []
+        windows = []
         for b in range(blocks):
             block = slice(b * P, (b + 1) * P)
-            values = held.tile([P, places], F32, name="values")
-            gates = held.tile([P, places], F32, name="gates")
-            stream = held.tile([P, n], F32, name="stream")
-            early = n - PIECE if b == blocks - 1 else n
+            values = per_block.tile([P, places], F32, name="values")
+            gates = per_block.tile([P, places], F32, name="gates")
             nc.sync.dma_start(values[:], tab[0, block, :])
-            nc.sync.dma_start(stream[:, :early], y[block, :early])
+            if b == last:
+                nc.sync.dma_start(stream[:, b, : n - PIECE], y_blocks[:, b, : n - PIECE])
             nc.sync.dma_start(gates[:], tab[1, block, :])
-            if early < n:
-                nc.sync.dma_start(stream[:, early:], y[block, early:])
-            loaded.append((values, gates, stream))
+            windows.append((values, gates))
+        nc.sync.dma_start(stream[:, last, n - PIECE :], y_blocks[:, last, n - PIECE :])
 
-        for b, (values, gates, stream) in enumerate(loaded):
-            block = slice(b * P, (b + 1) * P)
-            clipped = held.tile([P, n], F32, name="clipped")
-            gated = held.tile([P, n], F32, name="gated")
-            product = held.tile([P, n], F32, name="product")
+        for b, (values, gates) in enumerate(windows):
+            clipped = per_block.tile([P, n], F32, name="clipped")
+            gated = per_block.tile([P, n], F32, name="gated")
             for cols in pieces:
                 entries = offsets[:, cols.start // LIST_ROWS : cols.stop // LIST_ROWS]
-                nc.vector.tensor_tensor(clipped[:, cols], values[:].indirect(entries), stream[:, cols], MIN)
+                nc.vector.tensor_tensor(clipped[:, cols], values[:].indirect(entries), stream[:, b, cols], MIN)
                 nc.scalar.activation(gated[:, cols], gates[:].indirect(entries), SILU)
             for cols in pieces:
-                nc.vector.tensor_tensor(product[:, cols], clipped[:, cols], gated[:, cols], MULT)
-            for cols in pieces if b == blocks - 1 else [slice(0, n)]:
-                nc.sync.dma_start(out[block, cols], product[:, cols])
+                nc.vector.tensor_tensor(product[:, b, cols], clipped[:, cols], gated[:, cols], MULT)
+
+        nc.sync.dma_start(out_blocks[:, :last, :], product[:, :last, :])
+        for cols in pieces:
+            nc.sync.dma_start(out_blocks[:, last, cols], product[:, last, cols])

import concourse.mybir as mybir

F32 = mybir.dt.float32
U16 = mybir.dt.uint16
MIN = mybir.AluOpType.min
MULT = mybir.AluOpType.mult
SILU = mybir.ActivationFunctionType.Silu

P = 128
LIST_ROWS = 16
PIECE = 512


def tile_lookup_vg_minsilu_out_kernel(tc, tab, y, offs, out):
    nc = tc.nc
    rows, places = tab.shape[1], tab.shape[2]
    n = y.shape[1]
    blocks = rows // P
    last = blocks - 1
    pieces = [slice(start, start + PIECE) for start in range(0, n, PIECE)]
    y_blocks = y.rearrange("(b p) j -> p b j", p=P)
    out_blocks = out.rearrange("(b p) j -> p b j", p=P)

    with (
        tc.tile_pool(name="held", bufs=1) as held,
        tc.tile_pool(name="per_block", bufs=blocks) as per_block,
    ):
        offsets = held.tile([P, n // LIST_ROWS], U16, name="offsets")
        stream = held.tile([P, blocks, n], F32, name="stream")
        product = held.tile([P, blocks, n], F32, name="product")
        nc.sync.dma_start(offsets[:], offs)
        nc.scalar.dma_start(stream[:, :last, :], y_blocks[:, :last, :])

        windows = []
        for b in range(blocks):
            block = slice(b * P, (b + 1) * P)
            values = per_block.tile([P, places], F32, name="values")
            gates = per_block.tile([P, places], F32, name="gates")
            nc.sync.dma_start(values[:], tab[0, block, :])
            if b == last:
                nc.sync.dma_start(stream[:, b, : n - PIECE], y_blocks[:, b, : n - PIECE])
            nc.sync.dma_start(gates[:], tab[1, block, :])
            windows.append((values, gates))
        nc.sync.dma_start(stream[:, last, n - PIECE :], y_blocks[:, last, n - PIECE :])

        for b, (values, gates) in enumerate(windows):
            clipped = per_block.tile([P, n], F32, name="clipped")
            gated = per_block.tile([P, n], F32, name="gated")
            for cols in pieces:
                entries = offsets[:, cols.start // LIST_ROWS : cols.stop // LIST_ROWS]
                nc.vector.tensor_tensor(clipped[:, cols], values[:].indirect(entries), stream[:, b, cols], MIN)
                nc.scalar.activation(gated[:, cols], gates[:].indirect(entries), SILU)
            for cols in pieces:
                nc.vector.tensor_tensor(product[:, b, cols], clipped[:, cols], gated[:, cols], MULT)

        nc.sync.dma_start(out_blocks[:, :last, :], product[:, :last, :])
        for cols in pieces:
            nc.sync.dma_start(out_blocks[:, last, cols], product[:, last, cols])
